import numpy as np
import ml_dtypes


def mxq(x, axis, fmt="e4m3"):
    dtype, down = {"e4m3": (ml_dtypes.float8_e4m3fn, 7), "e5m2": (ml_dtypes.float8_e5m2, 14)}[fmt]
    v = np.moveaxis(np.asarray(x, np.float32).astype(ml_dtypes.bfloat16).astype(np.float64), axis, -1)
    blocks = v.reshape(v.shape[:-1] + (-1, 32))
    amax = np.abs(blocks).max(-1, keepdims=True)
    byte = np.maximum(np.where(amax > 0, np.frexp(amax)[1] - 1 + 127, 0) - down, 1)
    scale = np.exp2(byte - 127.0)
    codes = (blocks / scale).astype(np.float32).astype(dtype).astype(np.float64)
    return np.moveaxis((codes * scale).reshape(v.shape), -1, axis)


WIDE = False


def mx_kscale(k):
    if not WIDE:
        return np.ones(k)
    levels = np.array([10, -10, 5, -5, 0])
    if k % 512:
        return np.exp2(np.random.permutation(np.resize(levels, k // 32))).repeat(32)
    a = np.empty((k // 512, 16))
    for p in range(k // 512):
        a[p, :8] = np.random.permutation(np.resize(levels, 8))
        for g in range(8):
            far = levels[np.abs(levels - a[p, g]) >= 10]
            a[p, g + 8] = far[np.random.randint(len(far))]
    return np.exp2(a.ravel()).repeat(32)


def f64(x):
    return np.asarray(x).astype(np.float64)


def striped(idx):
    return np.tile(np.asarray(idx).reshape(-1, 16).T, (8, 1)).astype(np.uint16)


def unstriped(offs):
    return offs[:16].T.reshape(-1).astype(np.int64)


E2M1 = np.array([0.0, 0.5, 1.0, 1.5, 2.0, 3.0, 4.0, 6.0, -0.0, -0.5, -1.0, -1.5, -2.0, -3.0, -4.0, -6.0])


def pack_weight(w, fmt):
    k, n = w.shape
    w = f64(np.asarray(w, np.float32).astype(ml_dtypes.bfloat16)).reshape(k // 32, 32, n)
    amax = np.abs(w).max(1)
    if fmt == "e4m3":
        byte = np.frexp(amax)[1] - 1 + 127 - 7
    else:
        mant, ex = np.frexp(amax / 6.0)
        byte = np.where(mant > 0.5, ex, ex - 1) + 127
    byte = np.clip(np.where(amax > 0, byte, 1), 1, 254)
    scaled = (w * np.exp2(127.0 - byte)[:, None, :]).reshape(k, n).astype(np.float32)
    by_word = np.ascontiguousarray(scaled.reshape(k // 512, 128, 4, n).transpose(0, 1, 3, 2))
    if fmt == "e4m3":
        words = by_word.astype(ml_dtypes.float8_e4m3fn).view(np.uint8)
    else:
        c = by_word.astype(ml_dtypes.float4_e2m1fn).view(np.uint8) & 0xF
        words = (c[..., 0::2] | (c[..., 1::2] << 4)).reshape(k // 512, 128, 2 * n)
    return np.ascontiguousarray(words), np.ascontiguousarray(byte.astype(np.uint8).reshape(k // 512, 16, n))


def unpack_weight(words, scales, fmt):
    g, _, n = scales.shape
    words = np.ascontiguousarray(words).reshape(g, 128, n, -1)
    if fmt == "e4m3":
        vals = words.view(ml_dtypes.float8_e4m3fn).astype(np.float64)
    else:
        nib = np.empty((g, 128, n, 4), np.uint8)
        nib[..., 0::2] = words & 0xF
        nib[..., 1::2] = words >> 4
        vals = E2M1[nib]
    vals = vals * np.repeat(np.exp2(scales.astype(np.float64) - 127.0), 8, axis=1)[..., None]
    return vals.transpose(0, 1, 3, 2).reshape(g * 512, n)


K, T, J, I, N = 512, 2048, 1024, 512, 512


def setup_inputs():
    n = np.random.standard_normal
    idx = np.random.permutation(T)[:J]
    fk = mx_kscale(K)
    wap = pack_weight(n((K, N)) * 1 / np.sqrt(K) * fk[:, None], "e2m1")
    wbp = pack_weight(n((K, N)) * 1 / np.sqrt(K) * fk[:, None], "e4m3")
    return {
        "xf": (n((K, T)) / fk[:, None]).astype(np.float32),
        "wa_words": wap[0],
        "wa_scales": wap[1],
        "wb_words": wbp[0],
        "wb_scales": wbp[1],
        "rw": (np.random.uniform(0.5, 2.0, (1, J))).astype(np.float32),
        "offs": striped(idx),
    }


def reference(xf, wa_words, wa_scales, wb_words, wb_scales, rw, offs):
    idx = unstriped(offs)
    wau = unpack_weight(wa_words, wa_scales, "e2m1")
    wbu = unpack_weight(wb_words, wb_scales, "e4m3")
    xg = f64(xf)[:, idx]
    xa = xg[:, 0:0 + I]
    xb = xg[:, 512:512 + I]
    xaq = mxq(xa, 0, "e4m3")
    za = wau.T @ xaq
    xbq = mxq(xb, 0, "e4m3")
    zb = wbu.T @ xbq
    z = np.concatenate([za, zb], axis=1)
    y = np.maximum(z, 0.0) * f64(rw)
    return y

@@ -1,0 +1,146 @@
+from contextlib import ExitStack
+
+import concourse.mybir as mybir
+from concourse.masks import make_identity
+
+K, T, J, N = 512, 2048, 1024, 512
+FLOPS = 2 * K * N * J
+
+F32 = mybir.dt.float32
+BF16 = mybir.dt.bfloat16
+I32 = mybir.dt.int32
+U32 = mybir.dt.uint32
+U16 = mybir.dt.uint16
+U8 = mybir.dt.uint8
+FP8X4 = mybir.dt.float8_e4m3fn_x4
+FP4X4 = mybir.dt.float4_e2m1fn_x4
+ALU = mybir.AluOpType
+
+P = 128
+PACK = 4
+CHUNK = 256
+CHUNKS = J // CHUNK
+HALF = J // 2
+NB = N // P
+BANK = 512
+RW_RUN = J // P
+
+
+def tile_list_halves_of_the_list_kernel(tc, xf, wa_words, wa_scales, wb_words, wb_scales, rw, offs, out):
+    nc = tc.nc
+    with ExitStack() as ctx:
+        keep = ctx.enter_context(tc.tile_pool(name="keep", bufs=1))
+        psum = ctx.enter_context(tc.psum_pool(name="psum", bufs=1))
+
+        offsets = keep.tile([P, J // 16], U16, name="offsets")
+        nc.sync.dma_start(offsets[:], offs)
+
+        w_scales = keep.tile([P, 2 * N], U8, name="w_scales", align_bytes=64)
+        nc.vector.memset(w_scales[:].bitcast(I32), 0)
+        ident = keep.tile([P, P], F32, name="ident")
+        make_identity(nc, ident[:])
+
+        rows = xf.rearrange("(p t) c -> t p c", t=PACK)
+        planes = [keep.tile([P, T], F32, name=f"plane{t}") for t in range(PACK)]
+        for t in range(PACK - 1):
+            nc.sync.dma_start(planes[t][:], rows[t])
+        rw_cols = keep.tile([P, RW_RUN], F32, name="rw_cols")
+        nc.sync.dma_start(rw_cols[:], rw.rearrange("o (p b) -> (o p) b", b=RW_RUN))
+        nc.sync.dma_start(planes[PACK - 1][:], rows[PACK - 1])
+
+        wa_codes = keep.tile([P, 2 * N], U8, name="wa_codes", align_bytes=64)
+        nc.sync.dma_start(wa_codes[:].bitcast(I32), wa_words[0].bitcast(I32))
+        wb_codes = keep.tile([P, N], U32, name="wb_codes", align_bytes=64)
+        nc.sync.dma_start(wb_codes[:].bitcast(I32), wb_words[0].rearrange("p n r -> p (n r)").bitcast(I32))
+        for h, scales in enumerate((wa_scales, wb_scales)):
+            for q in range(4):
+                nc.sync.dma_start(
+                    w_scales[32 * q : 32 * q + 4, h * N : (h + 1) * N].bitcast(I32),
+                    scales[0, 4 * q : 4 * q + 4, :].bitcast(I32),
+                )
+
+        banks = [psum.tile([P, BANK], F32, name=f"bank{b}") for b in range(8)]
+
+        rw_all = keep.tile([P, J], F32, name="rw_all")
+        for u in range(2):
+            bank = banks[6 + u]
+            for b in range(4):
+                col = 4 * u + b
+                nc.tensor.transpose(bank[:, b * P : (b + 1) * P], rw_cols[:, col : col + 1].to_broadcast([P, P]), ident[:])
+            nc.scalar.copy(
+                rw_all[:].rearrange("m (p b) -> m p b", b=RW_RUN)[:, :, 4 * u : 4 * u + 4],
+                bank[:].rearrange("m (b p) -> m p b", b=4),
+            )
+
+        picked = keep.tile([P, PACK * J + (PACK - 1) * CHUNK], BF16, name="picked", align_bytes=64)
+        by_plane = picked[:, 0 : PACK * J].rearrange("p (t j) -> p t j", t=PACK)
+
+        def gather(t, j0, j1):
+            nc.vector.tensor_copy(picked[:, t * J + j0 : t * J + j1], planes[t][:].indirect(offsets[:, j0 // 16 : j1 // 16]))
+
+        woven = [picked[:, PACK * J - CHUNK :]]
+        woven = woven + [keep.tile([P, PACK * CHUNK], BF16, name=f"woven{c}", align_bytes=64)[:] for c in range(1, CHUNKS)]
+        x_codes = [keep.tile([P, CHUNK], U32, name=f"x_codes{c}", align_bytes=64) for c in range(CHUNKS)]
+        x_scales = [keep.tile([P, CHUNK], U8, name=f"x_scales{c}", align_bytes=64) for c in range(CHUNKS)]
+
+        def weave(c, j0, j1):
+            nc.scalar.copy(
+                woven[c][:, PACK * (j0 - c * CHUNK) : PACK * (j1 - c * CHUNK)].rearrange("p (g i t) -> p g t i", i=4, t=PACK),
+                by_plane[:, :, j0:j1].rearrange("p t (g i) -> p g t i", i=4),
+            )
+
+        def quantize_and_multiply(c):
+            nc.vector.quantize_mx(out=x_codes[c][:].bitcast(FP8X4), scales=x_scales[c][:], in_=woven[c])
+            h = c * CHUNK // HALF
+            for nb in range(NB):
+                if h == 0:
+                    lhsT = wa_codes[:, 2 * P * nb : 2 * P * (nb + 1)].bitcast(FP4X4)
+                    acc = banks[2 * c + nb // 2][:, (nb % 2) * CHUNK : (nb % 2 + 1) * CHUNK]
+                else:
+                    lhsT = wb_codes[:, P * nb : P * (nb + 1)].bitcast(FP8X4)
+                    acc = banks[4 + nb][:, (c % 2) * CHUNK : (c % 2 + 1) * CHUNK]
+                nc.tensor.matmul_mx(
+                    out=acc,
+                    lhsT=lhsT,
+                    lhsT_scale=w_scales[:, h * N + P * nb : h * N + P * (nb + 1)],
+                    rhs=x_codes[c][:].bitcast(FP8X4),
+                    rhs_scale=x_scales[c][:],
+                    start=True,
+                    stop=True,
+                )
+
+        out_blocks = out.rearrange("(b p) j -> p b j", p=P)
+
+        def finish(b):
+            result = keep.tile([P, BANK], F32, name=f"result{b}")
+            if b < 4:
+                c, u = divmod(b, 2)
+                cols = slice(c * CHUNK, (c + 1) * CHUNK)
+                res = result[:].rearrange("p (b j) -> p b j", b=2)
+                acc = banks[b][:].rearrange("p (b j) -> p b j", b=2)
+                weight = rw_all[:, cols].unsqueeze(1).to_broadcast([P, 2, CHUNK])
+                dest = out_blocks[:, 2 * u : 2 * u + 2, cols]
+            else:
+                res, acc, weight = result[:], banks[b][:], rw_all[:, HALF:J]
+                dest = out_blocks[:, b - 4, HALF:J]
+            nc.vector.scalar_tensor_tensor(out=res, in0=acc, scalar=0.0, in1=weight, op0=ALU.max, op1=ALU.mult)
+            nc.sync.dma_start(dest, res)
+
+        for t in range(PACK - 1):
+            gather(t, 0, J)
+        last = PACK - 1
+        gather(last, 0, CHUNK // 2)
+        weave(0, 0, CHUNK // 2)
+        gather(last, CHUNK // 2, CHUNK)
+        weave(0, CHUNK // 2, CHUNK)
+        for c in range(1, CHUNKS - 1):
+            gather(last, c * CHUNK, (c + 1) * CHUNK)
+            weave(c, c * CHUNK, (c + 1) * CHUNK)
+        quantize_and_multiply(0)
+        gather(last, J - CHUNK, J)
+        weave(CHUNKS - 1, J - CHUNK, J)
+        for c in range(1, CHUNKS):
+            quantize_and_multiply(c)
+            finish(c - 1)
+        for b in range(CHUNKS - 1, 8):
+            finish(b)

@@ -32,27 +32,27 @@ def tile_list_halves_of_the_list_kernel(tc, xf, wa_words, wa_scales, wb_words, w
         keep = ctx.enter_context(tc.tile_pool(name="keep", bufs=1))
         psum = ctx.enter_context(tc.psum_pool(name="psum", bufs=1))
 
+        rw_rows = keep.tile([P, P], F32, name="rw_rows")
+        nc.gpsimd.memset(rw_rows[:], 0.0)
+        rows = xf.rearrange("(p t) c -> t p c", t=PACK)
+        planes = [keep.tile([P, T], F32, name=f"plane{t}") for t in range(PACK)]
+        nc.sync.dma_start(planes[0][:], rows[0])
         offsets = keep.tile([P, J // 16], U16, name="offsets")
         nc.sync.dma_start(offsets[:], offs)
+        nc.sync.dma_start(rw_rows[0:RW_RUN, :], rw.rearrange("o (b m) -> (o b) m", m=P))
+        for t in range(1, PACK):
+            nc.sync.dma_start(planes[t][:], rows[t])
 
         w_scales = keep.tile([P, 2 * N], U8, name="w_scales", align_bytes=64)
         nc.vector.memset(w_scales[:].bitcast(I32), 0)
         ident = keep.tile([P, P], F32, name="ident")
         make_identity(nc, ident[:])
 
-        rows = xf.rearrange("(p t) c -> t p c", t=PACK)
-        planes = [keep.tile([P, T], F32, name=f"plane{t}") for t in range(PACK)]
-        for t in range(PACK - 1):
-            nc.sync.dma_start(planes[t][:], rows[t])
-        rw_cols = keep.tile([P, RW_RUN], F32, name="rw_cols")
-        nc.sync.dma_start(rw_cols[:], rw.rearrange("o (p b) -> (o p) b", b=RW_RUN))
-        nc.sync.dma_start(planes[PACK - 1][:], rows[PACK - 1])
-
         wa_codes = keep.tile([P, 2 * N], U8, name="wa_codes", align_bytes=64)
-        nc.sync.dma_start(wa_codes[:].bitcast(I32), wa_words[0].bitcast(I32))
         wb_codes = keep.tile([P, N], U32, name="wb_codes", align_bytes=64)
-        nc.sync.dma_start(wb_codes[:].bitcast(I32), wb_words[0].rearrange("p n r -> p (n r)").bitcast(I32))
-        for h, scales in enumerate((wa_scales, wb_scales)):
+        wb_rows = wb_words[0].rearrange("p n r -> p (n r)")
+        for h, (codes, words, scales) in enumerate(((wa_codes, wa_words[0], wa_scales), (wb_codes, wb_rows, wb_scales))):
+            nc.sync.dma_start(codes[:].bitcast(I32), words.bitcast(I32))
             for q in range(4):
                 nc.sync.dma_start(
                     w_scales[32 * q : 32 * q + 4, h * N : (h + 1) * N].bitcast(I32),
@@ -61,16 +61,16 @@ def tile_list_halves_of_the_list_kernel(tc, xf, wa_words, wa_scales, wb_words, w
 
         banks = [psum.tile([P, BANK], F32, name=f"bank{b}") for b in range(8)]
 
+        nc.tensor.transpose(banks[5][:, 0:P], rw_rows[:], ident[:])
+        rw_cols = keep.tile([P, RW_RUN], F32, name="rw_cols")
+        nc.scalar.copy(rw_cols[:], banks[5][:, 0:RW_RUN])
         rw_all = keep.tile([P, J], F32, name="rw_all")
         for u in range(2):
             bank = banks[6 + u]
             for b in range(4):
                 col = 4 * u + b
                 nc.tensor.transpose(bank[:, b * P : (b + 1) * P], rw_cols[:, col : col + 1].to_broadcast([P, P]), ident[:])
-            nc.scalar.copy(
-                rw_all[:].rearrange("m (p b) -> m p b", b=RW_RUN)[:, :, 4 * u : 4 * u + 4],
-                bank[:].rearrange("m (b p) -> m p b", b=4),
-            )
+            nc.scalar.copy(rw_all[:, u * HALF : (u + 1) * HALF], bank[:])
 
         picked = keep.tile([P, PACK * J + (PACK - 1) * CHUNK], BF16, name="picked", align_bytes=64)
         by_plane = picked[:, 0 : PACK * J].rearrange("p (t j) -> p t j", t=PACK)

from contextlib import ExitStack

import concourse.mybir as mybir
from concourse.masks import make_identity

K, T, J, N = 512, 2048, 1024, 512
FLOPS = 2 * K * N * J

F32 = mybir.dt.float32
BF16 = mybir.dt.bfloat16
I32 = mybir.dt.int32
U32 = mybir.dt.uint32
U16 = mybir.dt.uint16
U8 = mybir.dt.uint8
FP8X4 = mybir.dt.float8_e4m3fn_x4
FP4X4 = mybir.dt.float4_e2m1fn_x4
ALU = mybir.AluOpType

P = 128
PACK = 4
CHUNK = 256
CHUNKS = J // CHUNK
HALF = J // 2
NB = N // P
BANK = 512
RW_RUN = J // P


def tile_list_halves_of_the_list_kernel(tc, xf, wa_words, wa_scales, wb_words, wb_scales, rw, offs, out):
    nc = tc.nc
    with ExitStack() as ctx:
        keep = ctx.enter_context(tc.tile_pool(name="keep", bufs=1))
        psum = ctx.enter_context(tc.psum_pool(name="psum", bufs=1))

        rw_rows = keep.tile([P, P], F32, name="rw_rows")
        nc.gpsimd.memset(rw_rows[:], 0.0)
        rows = xf.rearrange("(p t) c -> t p c", t=PACK)
        planes = [keep.tile([P, T], F32, name=f"plane{t}") for t in range(PACK)]
        nc.sync.dma_start(planes[0][:], rows[0])
        offsets = keep.tile([P, J // 16], U16, name="offsets")
        nc.sync.dma_start(offsets[:], offs)
        nc.sync.dma_start(rw_rows[0:RW_RUN, :], rw.rearrange("o (b m) -> (o b) m", m=P))
        for t in range(1, PACK):
            nc.sync.dma_start(planes[t][:], rows[t])

        w_scales = keep.tile([P, 2 * N], U8, name="w_scales", align_bytes=64)
        nc.vector.memset(w_scales[:].bitcast(I32), 0)
        ident = keep.tile([P, P], F32, name="ident")
        make_identity(nc, ident[:])

        wa_codes = keep.tile([P, 2 * N], U8, name="wa_codes", align_bytes=64)
        wb_codes = keep.tile([P, N], U32, name="wb_codes", align_bytes=64)
        wb_rows = wb_words[0].rearrange("p n r -> p (n r)")
        for h, (codes, words, scales) in enumerate(((wa_codes, wa_words[0], wa_scales), (wb_codes, wb_rows, wb_scales))):
            nc.sync.dma_start(codes[:].bitcast(I32), words.bitcast(I32))
            for q in range(4):
                nc.sync.dma_start(
                    w_scales[32 * q : 32 * q + 4, h * N : (h + 1) * N].bitcast(I32),
                    scales[0, 4 * q : 4 * q + 4, :].bitcast(I32),
                )

        banks = [psum.tile([P, BANK], F32, name=f"bank{b}") for b in range(8)]

        nc.tensor.transpose(banks[5][:, 0:P], rw_rows[:], ident[:])
        rw_cols = keep.tile([P, RW_RUN], F32, name="rw_cols")
        nc.scalar.copy(rw_cols[:], banks[5][:, 0:RW_RUN])
        rw_all = keep.tile([P, J], F32, name="rw_all")
        for u in range(2):
            bank = banks[6 + u]
            for b in range(4):
                col = 4 * u + b
                nc.tensor.transpose(bank[:, b * P : (b + 1) * P], rw_cols[:, col : col + 1].to_broadcast([P, P]), ident[:])
            nc.scalar.copy(rw_all[:, u * HALF : (u + 1) * HALF], bank[:])

        picked = keep.tile([P, PACK * J + (PACK - 1) * CHUNK], BF16, name="picked", align_bytes=64)
        by_plane = picked[:, 0 : PACK * J].rearrange("p (t j) -> p t j", t=PACK)

        def gather(t, j0, j1):
            nc.vector.tensor_copy(picked[:, t * J + j0 : t * J + j1], planes[t][:].indirect(offsets[:, j0 // 16 : j1 // 16]))

        woven = [picked[:, PACK * J - CHUNK :]]
        woven = woven + [keep.tile([P, PACK * CHUNK], BF16, name=f"woven{c}", align_bytes=64)[:] for c in range(1, CHUNKS)]
        x_codes = [keep.tile([P, CHUNK], U32, name=f"x_codes{c}", align_bytes=64) for c in range(CHUNKS)]
        x_scales = [keep.tile([P, CHUNK], U8, name=f"x_scales{c}", align_bytes=64) for c in range(CHUNKS)]

        def weave(c, j0, j1):
            nc.scalar.copy(
                woven[c][:, PACK * (j0 - c * CHUNK) : PACK * (j1 - c * CHUNK)].rearrange("p (g i t) -> p g t i", i=4, t=PACK),
                by_plane[:, :, j0:j1].rearrange("p t (g i) -> p g t i", i=4),
            )

        def quantize_and_multiply(c):
            nc.vector.quantize_mx(out=x_codes[c][:].bitcast(FP8X4), scales=x_scales[c][:], in_=woven[c])
            h = c * CHUNK // HALF
            for nb in range(NB):
                if h == 0:
                    lhsT = wa_codes[:, 2 * P * nb : 2 * P * (nb + 1)].bitcast(FP4X4)
                    acc = banks[2 * c + nb // 2][:, (nb % 2) * CHUNK : (nb % 2 + 1) * CHUNK]
                else:
                    lhsT = wb_codes[:, P * nb : P * (nb + 1)].bitcast(FP8X4)
                    acc = banks[4 + nb][:, (c % 2) * CHUNK : (c % 2 + 1) * CHUNK]
                nc.tensor.matmul_mx(
                    out=acc,
                    lhsT=lhsT,
                    lhsT_scale=w_scales[:, h * N + P * nb : h * N + P * (nb + 1)],
                    rhs=x_codes[c][:].bitcast(FP8X4),
                    rhs_scale=x_scales[c][:],
                    start=True,
                    stop=True,
                )

        out_blocks = out.rearrange("(b p) j -> p b j", p=P)

        def finish(b):
            result = keep.tile([P, BANK], F32, name=f"result{b}")
            if b < 4:
                c, u = divmod(b, 2)
                cols = slice(c * CHUNK, (c + 1) * CHUNK)
                res = result[:].rearrange("p (b j) -> p b j", b=2)
                acc = banks[b][:].rearrange("p (b j) -> p b j", b=2)
                weight = rw_all[:, cols].unsqueeze(1).to_broadcast([P, 2, CHUNK])
                dest = out_blocks[:, 2 * u : 2 * u + 2, cols]
            else:
                res, acc, weight = result[:], banks[b][:], rw_all[:, HALF:J]
                dest = out_blocks[:, b - 4, HALF:J]
            nc.vector.scalar_tensor_tensor(out=res, in0=acc, scalar=0.0, in1=weight, op0=ALU.max, op1=ALU.mult)
            nc.sync.dma_start(dest, res)

        for t in range(PACK - 1):
            gather(t, 0, J)
        last = PACK - 1
        gather(last, 0, CHUNK // 2)
        weave(0, 0, CHUNK // 2)
        gather(last, CHUNK // 2, CHUNK)
        weave(0, CHUNK // 2, CHUNK)
        for c in range(1, CHUNKS - 1):
            gather(last, c * CHUNK, (c + 1) * CHUNK)
            weave(c, c * CHUNK, (c + 1) * CHUNK)
        quantize_and_multiply(0)
        gather(last, J - CHUNK, J)
        weave(CHUNKS - 1, J - CHUNK, J)
        for c in range(1, CHUNKS):
            quantize_and_multiply(c)
            finish(c - 1)
        for b in range(CHUNKS - 1, 8):
            finish(b)
